import numpy as np
import ml_dtypes


def mxq(x, axis, fmt="e4m3"):
    dtype, down = {"e4m3": (ml_dtypes.float8_e4m3fn, 7), "e5m2": (ml_dtypes.float8_e5m2, 14)}[fmt]
    v = np.moveaxis(np.asarray(x, np.float32).astype(ml_dtypes.bfloat16).astype(np.float64), axis, -1)
    blocks = v.reshape(v.shape[:-1] + (-1, 32))
    amax = np.abs(blocks).max(-1, keepdims=True)
    byte = np.maximum(np.where(amax > 0, np.frexp(amax)[1] - 1 + 127, 0) - down, 1)
    scale = np.exp2(byte - 127.0)
    codes = (blocks / scale).astype(np.float32).astype(dtype).astype(np.float64)
    return np.moveaxis((codes * scale).reshape(v.shape), -1, axis)


WIDE = False


def mx_kscale(k, group=512):
    if not WIDE:
        return np.ones(k)
    levels = np.array([10, -10, 5, -5, 0])
    if group != 512:
        return np.exp2(np.random.permutation(np.resize(levels, k // group))).repeat(group)
    if k % 512:
        return np.exp2(np.random.permutation(np.resize(levels, k // 32))).repeat(32)
    a = np.empty((k // 512, 16))
    for p in range(k // 512):
        a[p, :8] = np.random.permutation(np.resize(levels, 8))
        for g in range(8):
            far = levels[np.abs(levels - a[p, g]) >= 10]
            a[p, g + 8] = far[np.random.randint(len(far))]
    return np.exp2(a.ravel()).repeat(32)


def f64(x):
    return np.asarray(x).astype(np.float64)


E2M1 = np.array([0.0, 0.5, 1.0, 1.5, 2.0, 3.0, 4.0, 6.0, -0.0, -0.5, -1.0, -1.5, -2.0, -3.0, -4.0, -6.0])


def pack_group(w):
    k, n = w.shape
    w = f64(np.asarray(w, np.float32).astype(ml_dtypes.bfloat16)).reshape(k // 32, 32, n)
    amax = np.abs(w).max(1)
    mant, ex = np.frexp(amax / 6.0)
    byte = np.clip(np.where(amax > 0, np.where(mant > 0.5, ex, ex - 1) + 127, 1), 1, 254)
    scaled = (w * np.exp2(127.0 - byte)[:, None, :]).reshape(k, n).astype(np.float32)
    c = np.ascontiguousarray(scaled.reshape(k // 4, 4, n).transpose(0, 2, 1)).astype(ml_dtypes.float4_e2m1fn).view(np.uint8) & 0xF
    return np.ascontiguousarray((c[..., 0::2] | (c[..., 1::2] << 4)).reshape(k // 4, 2 * n)), byte.astype(np.uint8)


def unpack_group(words, scales):
    p, n = words.shape[0], scales.shape[1]
    words = np.ascontiguousarray(words).reshape(p, n, 2)
    nib = np.empty((p, n, 4), np.uint8)
    nib[..., 0::2] = words & 0xF
    nib[..., 1::2] = words >> 4
    return E2M1[nib].transpose(0, 2, 1).reshape(4 * p, n) * np.repeat(np.exp2(scales.astype(np.float64) - 127.0), 32, axis=0)


G, D, M, O, N = 2, 256, 256, 256, 512


def setup_inputs():
    n = np.random.standard_normal
    s_d = mx_kscale(D, 0)
    s_o = mx_kscale(O, 0)
    w1_ = [pack_group(w) for w in n((G, D, M)) / np.sqrt(D) / s_d[:, None]]
    w2_ = [pack_group(w) for w in n((G, D, M)) / np.sqrt(D) / s_d[:, None]]
    w3_ = [pack_group(w) for w in n((G, D, M)) / np.sqrt(D) / s_d[:, None]]
    wo_ = [pack_group(w) for w in n((G, O, M)) / np.sqrt(O) / s_o[:, None]]
    return {
        "x": (n((G, D, N)) * s_d[:, None]).astype(np.float32),
        "w1_words": np.stack([w[0] for w in w1_]),
        "w1_scales": np.stack([w[1] for w in w1_]),
        "w2_words": np.stack([w[0] for w in w2_]),
        "w2_scales": np.stack([w[1] for w in w2_]),
        "w3_words": np.stack([w[0] for w in w3_]),
        "w3_scales": np.stack([w[1] for w in w3_]),
        "wo_words": np.stack([w[0] for w in wo_]),
        "wo_scales": np.stack([w[1] for w in wo_]),
        "dy": (n((G, O, N)) * s_o[:, None]).astype(np.float32),
        "old": (0.3 * n((G, M, N))).astype(np.float32),
    }


def reference(x, w1_words, w1_scales, w2_words, w2_scales, w3_words, w3_scales, wo_words, wo_scales, dy, old):
    w1 = np.stack([unpack_group(w1_words[g], w1_scales[g]) for g in range(G)])
    xq = mxq(f64(x), 1, "e4m3")
    z1 = w1.transpose(0, 2, 1) @ xq
    w2 = np.stack([unpack_group(w2_words[g], w2_scales[g]) for g in range(G)])
    z2 = w2.transpose(0, 2, 1) @ xq
    w3 = np.stack([unpack_group(w3_words[g], w3_scales[g]) for g in range(G)])
    z3 = w3.transpose(0, 2, 1) @ xq
    se = np.exp(z1) + np.exp(z2) + np.exp(z3)
    wo = np.stack([unpack_group(wo_words[g], wo_scales[g]) for g in range(G)])
    dyq = mxq(f64(dy), 1, "e4m3")
    c0 = wo.transpose(0, 2, 1) @ dyq
    dse = c0 * np.tanh(z1) / se
    dz1 = c0 * np.log(se) * (1.0 - np.square(np.tanh(z1))) + dse * np.exp(z1)
    y = dz1 + f64(old)
    return y

@@ -1,0 +1,171 @@
+from contextlib import ExitStack
+
+import concourse.mybir as mybir
+
+G, D, M, N = 2, 256, 256, 512
+FLOPS = 4 * 2 * G * D * M * N
+
+F32 = mybir.dt.float32
+BF16 = mybir.dt.bfloat16
+I32 = mybir.dt.int32
+U32 = mybir.dt.uint32
+U8 = mybir.dt.uint8
+FP8X4 = mybir.dt.float8_e4m3fn_x4
+FP4X4 = mybir.dt.float4_e2m1fn_x4
+ACT = mybir.ActivationFunctionType
+ALU = mybir.AluOpType
+
+P = 128
+PACK = 4
+ROWS = D // PACK
+M_TILE = 128
+TILES = [(g, h) for h in range(M // M_TILE) for g in range(G)]
+SCALAR_COLS = 192
+W1, W2, W3, WO = range(4)
+
+
+def tile_rows_bsoftmaxthree_kernel(
+    tc, x, w1_words, w1_scales, w2_words, w2_scales, w3_words, w3_scales, wo_words, wo_scales, dy, old, out
+):
+    nc = tc.nc
+    words_in = [w1_words, w2_words, w3_words, wo_words]
+    scales_in = [w1_scales, w2_scales, w3_scales, wo_scales]
+    n_tiles = len(TILES)
+
+    with ExitStack() as ctx:
+        sb = ctx.enter_context(tc.tile_pool(name="sb", bufs=1))
+        ps = ctx.enter_context(tc.psum_pool(name="ps", bufs=1))
+        ctx.enter_context(tc.manual_schedule())
+
+        def per_tile(name):
+            return [sb.tile([P, N], F32, name="%s%d" % (name, i)) for i in range(n_tiles)]
+
+        x_raw = sb.tile([P, PACK, N], F32, name="x_raw")
+        dy_raw = sb.tile([P, PACK, N], F32, name="dy_raw")
+        x_bf = sb.tile([P, N, PACK], BF16, name="x_bf", align_bytes=64)
+        dy_bf = sb.tile([P, N, PACK], BF16, name="dy_bf", align_bytes=64)
+        x_codes = sb.tile([P, N], U32, name="x_codes", align_bytes=64)
+        dy_codes = sb.tile([P, N], U32, name="dy_codes", align_bytes=64)
+        x_scale = sb.tile([P, N], U8, name="x_scale", align_bytes=64)
+        dy_scale = sb.tile([P, N], U8, name="dy_scale", align_bytes=64)
+        w_words = [sb.tile([P, 2 * M], U8, name="w_words%d" % w, align_bytes=64) for w in range(4)]
+        w_stage = sb.tile([16, 4 * M], U8, name="w_stage", align_bytes=64)
+        w_scale = sb.tile([P, 4 * M], U8, name="w_scale", align_bytes=64)
+        old_sb = [sb.tile([P, M // M_TILE, N], F32, name="old%d" % g) for g in range(G)]
+        banks = [[ps.tile([P, N], F32, name="bank%d_%d" % (g, w)) for w in range(4)] for g in range(G)]
+        e1, e2, e3, th, th2 = [per_tile(name) for name in ("e1", "e2", "e3", "th", "th2")]
+        s23, se, ct, cte, cs = [per_tile(name) for name in ("s23", "se", "ct", "cte", "cs")]
+        lse, csl, rest, inv, term, res = [per_tile(name) for name in ("lse", "csl", "rest", "inv", "term", "res")]
+
+        def load_words(eng, w):
+            eng.dma_start(out=w_words[w][:].bitcast(I32), in_=words_in[w].rearrange("g p b -> (g p) b").bitcast(I32))
+
+        def load_rows(tile, src):
+            nc.sync.dma_start(out=tile[:], in_=src.rearrange("g (p j) n -> (g p) j n", j=PACK))
+
+        nc.vector.memset(w_scale[:].bitcast(U32), 0)
+        for w in range(4):
+            nc.scalar.dma_start(
+                out=w_stage[:, w * M : (w + 1) * M].bitcast(I32),
+                in_=scales_in[w].rearrange("g t m -> (g t) m").bitcast(I32),
+            )
+        for w in (W2, W3, W1):
+            load_words(nc.scalar, w)
+        load_rows(x_raw, x)
+        for q in range(4):
+            nc.sync.dma_start(
+                out=w_scale[32 * q : 32 * q + 4, :].bitcast(I32), in_=w_stage[4 * q : 4 * q + 4, :].bitcast(I32)
+            )
+        load_rows(dy_raw, dy)
+        load_words(nc.sync, WO)
+        for g in range(G):
+            nc.sync.dma_start(out=old_sb[g][:], in_=old[g].rearrange("(h p) n -> p h n", p=M_TILE))
+
+        def quantize(codes, scale, packed):
+            nc.vector.quantize_mx(
+                out=codes[:].bitcast(FP8X4), scales=scale[:], in_=packed[:].rearrange("p n j -> p (n j)")
+            )
+
+        def product(i, w):
+            g, h = TILES[i]
+            rows = slice(ROWS * g, ROWS * (g + 1))
+            codes, scale = (dy_codes, dy_scale) if w == WO else (x_codes, x_scale)
+            nc.tensor.matmul_mx(
+                out=banks[g][w][:],
+                lhsT=w_words[w][rows, 2 * M_TILE * h : 2 * M_TILE * (h + 1)].bitcast(FP4X4),
+                lhsT_scale=w_scale[rows, w * M + M_TILE * h : w * M + M_TILE * (h + 1)],
+                rhs=codes[rows, :].bitcast(FP8X4),
+                rhs_scale=scale[rows, :],
+                start=True,
+                stop=True,
+            )
+
+        def forward(i):
+            bank = banks[TILES[i][0]]
+            for w in (W2, W3, W1):
+                product(i, w)
+            nc.scalar.activation(out=e2[i][:], in_=bank[W2][:], func=ACT.Exp)
+            nc.scalar.activation(out=e3[i][:], in_=bank[W3][:], func=ACT.Exp)
+            nc.scalar.activation(out=e1[i][:], in_=bank[W1][:], func=ACT.Exp)
+            nc.scalar.activation(out=th[i][:], in_=bank[W1][:], func=ACT.Tanh)
+            nc.scalar.activation(out=th2[i][:], in_=th[i][:], func=ACT.Square)
+
+        def tt(dst, a, b, op):
+            nc.vector.tensor_tensor(out=dst, in0=a, in1=b, op=op)
+
+        def with_c0(i):
+            c0 = banks[TILES[i][0]][WO]
+            tt(ct[i][:], c0[:], th[i][:], ALU.mult)
+            nc.vector.scalar_tensor_tensor(
+                out=cs[i][:], in0=th2[i][:], scalar=1.0, in1=c0[:], op0=ALU.subtract, op1=ALU.mult
+            )
+
+        x_t = x_raw[:].rearrange("p j n -> p n j")
+        nc.scalar.copy(out=x_bf[:, :SCALAR_COLS, :], in_=x_t[:, :SCALAR_COLS, :])
+        nc.vector.tensor_copy(out=x_bf[:, SCALAR_COLS:, :], in_=x_t[:, SCALAR_COLS:, :])
+        quantize(x_codes, x_scale, x_bf)
+        nc.vector.tensor_copy(out=dy_bf[:], in_=dy_raw[:].rearrange("p j n -> p n j"))
+
+        forward(0)
+        forward(1)
+        for i in range(n_tiles):
+            if i >= 2:
+                forward(i)
+            tt(s23[i][:], e2[i][:], e3[i][:], ALU.add)
+            if i == 0:
+                quantize(dy_codes, dy_scale, dy_bf)
+                product(0, WO)
+                product(1, WO)
+            else:
+                tt(cte[i - 1][:], ct[i - 1][:], e1[i - 1][:], ALU.mult)
+            tt(se[i][:], s23[i][:], e1[i][:], ALU.add)
+            if i >= 2:
+                product(i, WO)
+            with_c0(i)
+        tt(cte[-1][:], ct[-1][:], e1[-1][:], ALU.mult)
+
+        for i in range(n_tiles):
+            nc.scalar.activation(out=lse[i][:], in_=se[i][:], func=ACT.Ln)
+        for i in range(n_tiles):
+            nc.scalar.activation(out=inv[i][:], in_=lse[i][:], func=ACT.Exp, scale=-1.0)
+
+        def finish_rest(i):
+            g, h = TILES[i]
+            tt(rest[i][:], old_sb[g][:, h, :], csl[i][:], ALU.subtract)
+
+        for i in range(n_tiles):
+            tt(csl[i][:], cs[i][:], lse[i][:], ALU.mult)
+            if i >= 1:
+                finish_rest(i - 1)
+        finish_rest(n_tiles - 1)
+
+        def finish(i):
+            g, h = TILES[i]
+            tt(res[i][:], term[i][:], rest[i][:], ALU.add)
+            nc.sync.dma_start(out=out[g, M_TILE * h : M_TILE * (h + 1), :], in_=res[i][:])
+
+        for i in range(n_tiles):
+            tt(term[i][:], cte[i][:], inv[i][:], ALU.mult)
+            if i >= 1:
+                finish(i - 1)
+        finish(n_tiles - 1)

@@ -20,7 +20,8 @@ PACK = 4
 ROWS = D // PACK
 M_TILE = 128
 TILES = [(g, h) for h in range(M // M_TILE) for g in range(G)]
-SCALAR_COLS = 192
+HALF = N // 2
+SCALAR_COLS = 208
 W1, W2, W3, WO = range(4)
 
 
@@ -64,26 +65,34 @@ def tile_rows_bsoftmaxthree_kernel(
             nc.sync.dma_start(out=tile[:], in_=src.rearrange("g (p j) n -> (g p) j n", j=PACK))
 
         nc.vector.memset(w_scale[:].bitcast(U32), 0)
-        for w in range(4):
-            nc.scalar.dma_start(
+        for w, eng in ((W2, nc.sync), (W1, nc.scalar), (W3, nc.sync), (WO, nc.scalar)):
+            eng.dma_start(
                 out=w_stage[:, w * M : (w + 1) * M].bitcast(I32),
                 in_=scales_in[w].rearrange("g t m -> (g t) m").bitcast(I32),
             )
-        for w in (W2, W3, W1):
-            load_words(nc.scalar, w)
-        load_rows(x_raw, x)
-        for q in range(4):
+
+        def place_scales(q):
             nc.sync.dma_start(
                 out=w_scale[32 * q : 32 * q + 4, :].bitcast(I32), in_=w_stage[4 * q : 4 * q + 4, :].bitcast(I32)
             )
+
+        load_rows(x_raw, x)
+        for w in (W2, W3, W1):
+            load_words(nc.sync, w)
+        place_scales(0)
+        place_scales(1)
         load_rows(dy_raw, dy)
+        place_scales(2)
+        place_scales(3)
         load_words(nc.sync, WO)
         for g in range(G):
             nc.sync.dma_start(out=old_sb[g][:], in_=old[g].rearrange("(h p) n -> p h n", p=M_TILE))
 
-        def quantize(codes, scale, packed):
+        def quantize(codes, scale, packed, cols):
             nc.vector.quantize_mx(
-                out=codes[:].bitcast(FP8X4), scales=scale[:], in_=packed[:].rearrange("p n j -> p (n j)")
+                out=codes[:, cols].bitcast(FP8X4),
+                scales=scale[:, cols],
+                in_=packed[:, cols, :].rearrange("p n j -> p (n j)"),
             )
 
         def product(i, w):
@@ -122,8 +131,10 @@ def tile_rows_bsoftmaxthree_kernel(
 
         x_t = x_raw[:].rearrange("p j n -> p n j")
         nc.scalar.copy(out=x_bf[:, :SCALAR_COLS, :], in_=x_t[:, :SCALAR_COLS, :])
-        nc.vector.tensor_copy(out=x_bf[:, SCALAR_COLS:, :], in_=x_t[:, SCALAR_COLS:, :])
-        quantize(x_codes, x_scale, x_bf)
+        nc.vector.tensor_copy(out=x_bf[:, HALF:, :], in_=x_t[:, HALF:, :])
+        nc.vector.tensor_copy(out=x_bf[:, SCALAR_COLS:HALF, :], in_=x_t[:, SCALAR_COLS:HALF, :])
+        quantize(x_codes, x_scale, x_bf, slice(HALF, N))
+        quantize(x_codes, x_scale, x_bf, slice(0, HALF))
         nc.vector.tensor_copy(out=dy_bf[:], in_=dy_raw[:].rearrange("p j n -> p n j"))
 
         forward(0)
@@ -133,7 +144,7 @@ def tile_rows_bsoftmaxthree_kernel(
                 forward(i)
             tt(s23[i][:], e2[i][:], e3[i][:], ALU.add)
             if i == 0:
-                quantize(dy_codes, dy_scale, dy_bf)
+                quantize(dy_codes, dy_scale, dy_bf, slice(0, N))
                 product(0, WO)
                 product(1, WO)
             else:
@@ -159,13 +170,14 @@ def tile_rows_bsoftmaxthree_kernel(
                 finish_rest(i - 1)
         finish_rest(n_tiles - 1)
 
-        def finish(i):
+        def finish(i, cols):
             g, h = TILES[i]
-            tt(res[i][:], term[i][:], rest[i][:], ALU.add)
-            nc.sync.dma_start(out=out[g, M_TILE * h : M_TILE * (h + 1), :], in_=res[i][:])
+            tt(res[i][:, cols], term[i][:, cols], rest[i][:, cols], ALU.add)
+            nc.sync.dma_start(out=out[g, M_TILE * h : M_TILE * (h + 1), cols], in_=res[i][:, cols])
 
         for i in range(n_tiles):
             tt(term[i][:], cte[i][:], inv[i][:], ALU.mult)
             if i >= 1:
-                finish(i - 1)
-        finish(n_tiles - 1)
+                finish(i - 1, slice(0, N))
+        finish(n_tiles - 1, slice(0, HALF))
+        finish(n_tiles - 1, slice(HALF, N))

@@ -22,6 +22,7 @@ M_TILE = 128
 TILES = [(g, h) for h in range(M // M_TILE) for g in range(G)]
 HALF = N // 2
 SCALAR_COLS = 208
+RUN = 4
 W1, W2, W3, WO = range(4)
 
 
@@ -115,8 +116,8 @@ def tile_rows_bsoftmaxthree_kernel(
                 product(i, w)
             nc.scalar.activation(out=e2[i][:], in_=bank[W2][:], func=ACT.Exp)
             nc.scalar.activation(out=e3[i][:], in_=bank[W3][:], func=ACT.Exp)
-            nc.scalar.activation(out=e1[i][:], in_=bank[W1][:], func=ACT.Exp)
             nc.scalar.activation(out=th[i][:], in_=bank[W1][:], func=ACT.Tanh)
+            nc.scalar.activation(out=e1[i][:], in_=bank[W1][:], func=ACT.Exp)
             nc.scalar.activation(out=th2[i][:], in_=th[i][:], func=ACT.Square)
 
         def tt(dst, a, b, op):
@@ -129,13 +130,18 @@ def tile_rows_bsoftmaxthree_kernel(
                 out=cs[i][:], in0=th2[i][:], scalar=1.0, in1=c0[:], op0=ALU.subtract, op1=ALU.mult
             )
 
-        x_t = x_raw[:].rearrange("p j n -> p n j")
-        nc.scalar.copy(out=x_bf[:, :SCALAR_COLS, :], in_=x_t[:, :SCALAR_COLS, :])
-        nc.vector.tensor_copy(out=x_bf[:, HALF:, :], in_=x_t[:, HALF:, :])
-        nc.vector.tensor_copy(out=x_bf[:, SCALAR_COLS:HALF, :], in_=x_t[:, SCALAR_COLS:HALF, :])
+        def interleave(copy, packed, raw, cols):
+            copy(
+                out=packed[:, cols, :].rearrange("p (c i) j -> p c j i", i=RUN),
+                in_=raw[:, :, cols].rearrange("p j (c i) -> p c j i", i=RUN),
+            )
+
+        interleave(nc.scalar.copy, x_bf, x_raw, slice(0, SCALAR_COLS))
+        interleave(nc.vector.tensor_copy, x_bf, x_raw, slice(HALF, N))
+        interleave(nc.vector.tensor_copy, x_bf, x_raw, slice(SCALAR_COLS, HALF))
         quantize(x_codes, x_scale, x_bf, slice(HALF, N))
         quantize(x_codes, x_scale, x_bf, slice(0, HALF))
-        nc.vector.tensor_copy(out=dy_bf[:], in_=dy_raw[:].rearrange("p j n -> p n j"))
+        interleave(nc.vector.tensor_copy, dy_bf, dy_raw, slice(0, N))
 
         forward(0)
         forward(1)
@@ -175,9 +181,14 @@ def tile_rows_bsoftmaxthree_kernel(
             tt(res[i][:, cols], term[i][:, cols], rest[i][:, cols], ALU.add)
             nc.sync.dma_start(out=out[g, M_TILE * h : M_TILE * (h + 1), cols], in_=res[i][:, cols])
 
-        for i in range(n_tiles):
+        last = n_tiles - 1
+        halves = (slice(0, HALF), slice(HALF, N))
+        for i in range(last):
             tt(term[i][:], cte[i][:], inv[i][:], ALU.mult)
             if i >= 1:
                 finish(i - 1, slice(0, N))
-        finish(n_tiles - 1, slice(0, HALF))
-        finish(n_tiles - 1, slice(HALF, N))
+        finish(last - 1, slice(0, N))
+        for cols in halves:
+            tt(term[last][:, cols], cte[last][:, cols], inv[last][:, cols], ALU.mult)
+        for cols in halves:
+            finish(last, cols)

@@ -21,8 +21,9 @@ ROWS = D // PACK
 M_TILE = 128
 TILES = [(g, h) for h in range(M // M_TILE) for g in range(G)]
 HALF = N // 2
-SCALAR_COLS = 208
+SCALAR_COLS = 176
 RUN = 4
+ON_VECTOR = 1
 W1, W2, W3, WO = range(4)
 
 
@@ -43,7 +44,7 @@ def tile_rows_bsoftmaxthree_kernel(
             return [sb.tile([P, N], F32, name="%s%d" % (name, i)) for i in range(n_tiles)]
 
         x_raw = sb.tile([P, PACK, N], F32, name="x_raw")
-        dy_raw = sb.tile([P, PACK, N], F32, name="dy_raw")
+        dy_raw = [sb.tile([P, PACK, HALF], F32, name="dy_raw%d" % c) for c in range(2)]
         x_bf = sb.tile([P, N, PACK], BF16, name="x_bf", align_bytes=64)
         dy_bf = sb.tile([P, N, PACK], BF16, name="dy_bf", align_bytes=64)
         x_codes = sb.tile([P, N], U32, name="x_codes", align_bytes=64)
@@ -82,7 +83,8 @@ def tile_rows_bsoftmaxthree_kernel(
             load_words(nc.sync, w)
         place_scales(0)
         place_scales(1)
-        load_rows(dy_raw, dy)
+        load_rows(dy_raw[0], dy[:, :, :HALF])
+        load_rows(dy_raw[1], dy[:, :, HALF:])
         place_scales(2)
         place_scales(3)
         load_words(nc.sync, WO)
@@ -110,56 +112,75 @@ def tile_rows_bsoftmaxthree_kernel(
                 stop=True,
             )
 
-        def forward(i):
-            bank = banks[TILES[i][0]]
+        def forward_products(i):
             for w in (W2, W3, W1):
                 product(i, w)
+
+        def forward(i):
+            bank = banks[TILES[i][0]]
             nc.scalar.activation(out=e2[i][:], in_=bank[W2][:], func=ACT.Exp)
             nc.scalar.activation(out=e3[i][:], in_=bank[W3][:], func=ACT.Exp)
             nc.scalar.activation(out=th[i][:], in_=bank[W1][:], func=ACT.Tanh)
             nc.scalar.activation(out=e1[i][:], in_=bank[W1][:], func=ACT.Exp)
-            nc.scalar.activation(out=th2[i][:], in_=th[i][:], func=ACT.Square)
+            if i != ON_VECTOR:
+                nc.scalar.activation(out=th2[i][:], in_=th[i][:], func=ACT.Square)
 
         def tt(dst, a, b, op):
             nc.vector.tensor_tensor(out=dst, in0=a, in1=b, op=op)
 
-        def with_c0(i):
+        def slope(i):
             c0 = banks[TILES[i][0]][WO]
-            tt(ct[i][:], c0[:], th[i][:], ALU.mult)
-            nc.vector.scalar_tensor_tensor(
-                out=cs[i][:], in0=th2[i][:], scalar=1.0, in1=c0[:], op0=ALU.subtract, op1=ALU.mult
-            )
+            if i == ON_VECTOR:
+                tt(cs[i][:], th2[i][:], c0[:], ALU.subtract)
+            else:
+                nc.vector.scalar_tensor_tensor(
+                    out=cs[i][:], in0=th2[i][:], scalar=1.0, in1=c0[:], op0=ALU.subtract, op1=ALU.mult
+                )
 
         def interleave(copy, packed, raw, cols):
             copy(
                 out=packed[:, cols, :].rearrange("p (c i) j -> p c j i", i=RUN),
-                in_=raw[:, :, cols].rearrange("p j (c i) -> p c j i", i=RUN),
+                in_=raw.rearrange("p j (c i) -> p c j i", i=RUN),
             )
 
-        interleave(nc.scalar.copy, x_bf, x_raw, slice(0, SCALAR_COLS))
-        interleave(nc.vector.tensor_copy, x_bf, x_raw, slice(HALF, N))
-        interleave(nc.vector.tensor_copy, x_bf, x_raw, slice(SCALAR_COLS, HALF))
+        for copy, cols in (
+            (nc.scalar.copy, slice(0, SCALAR_COLS)),
+            (nc.vector.tensor_copy, slice(HALF, N)),
+            (nc.vector.tensor_copy, slice(SCALAR_COLS, HALF)),
+        ):
+            interleave(copy, x_bf, x_raw[:, :, cols], cols)
         quantize(x_codes, x_scale, x_bf, slice(HALF, N))
         quantize(x_codes, x_scale, x_bf, slice(0, HALF))
-        interleave(nc.vector.tensor_copy, dy_bf, dy_raw, slice(0, N))
+        for c in range(2):
+            cols = slice(c * HALF, (c + 1) * HALF)
+            interleave(nc.vector.tensor_copy, dy_bf, dy_raw[c][:], cols)
+            quantize(dy_codes, dy_scale, dy_bf, cols)
 
+        forward_products(0)
+        for i, w in ((1, W2), (0, WO), (1, W3), (1, W1), (1, WO)):
+            product(i, w)
         forward(0)
         forward(1)
+        forward_products(2)
+        forward_products(3)
+        forward(2)
+        forward(3)
         for i in range(n_tiles):
-            if i >= 2:
-                forward(i)
             tt(s23[i][:], e2[i][:], e3[i][:], ALU.add)
+            if i >= 1:
+                nc.gpsimd.tensor_tensor(out=se[i][:], in0=s23[i][:], in1=e1[i][:], op=ALU.add)
+            tt(ct[i][:], banks[TILES[i][0]][WO][:], th[i][:], ALU.mult)
             if i == 0:
-                quantize(dy_codes, dy_scale, dy_bf, slice(0, N))
-                product(0, WO)
-                product(1, WO)
+                tt(se[i][:], s23[i][:], e1[i][:], ALU.add)
             else:
-                tt(cte[i - 1][:], ct[i - 1][:], e1[i - 1][:], ALU.mult)
-            tt(se[i][:], s23[i][:], e1[i][:], ALU.add)
-            if i >= 2:
-                product(i, WO)
-            with_c0(i)
-        tt(cte[-1][:], ct[-1][:], e1[-1][:], ALU.mult)
+                slope(i - 1)
+                if i + 1 < n_tiles:
+                    product(i + 1, WO)
+            if i == n_tiles - 1:
+                slope(i)
+            if i == ON_VECTOR:
+                tt(th2[i][:], ct[i][:], th[i][:], ALU.mult)
+            tt(cte[i][:], ct[i][:], e1[i][:], ALU.mult)
 
         for i in range(n_tiles):
             nc.scalar.activation(out=lse[i][:], in_=se[i][:], func=ACT.Ln)

@@ -18,13 +18,18 @@ ALU = mybir.AluOpType
 P = 128
 PACK = 4
 ROWS = D // PACK
+QUADRANT = 32
+SCALE_ROWS = 4
 M_TILE = 128
-TILES = [(g, h) for h in range(M // M_TILE) for g in range(G)]
-HALF = N // 2
-SCALAR_COLS = 176
-RUN = 4
-ON_VECTOR = 1
 W1, W2, W3, WO = range(4)
+TILES = [(g, h) for g in range(G) for h in range(M // M_TILE)]
+LAST = len(TILES) - 1
+HALF = N // 2
+HALVES = (slice(0, HALF), slice(HALF, N))
+ALL = slice(0, N)
+RUN = 4
+SCALAR_COLS = 176
+SQUARE_ON_VECTOR = 1
 
 
 def tile_rows_bsoftmaxthree_kernel(
@@ -33,7 +38,6 @@ def tile_rows_bsoftmaxthree_kernel(
     nc = tc.nc
     words_in = [w1_words, w2_words, w3_words, wo_words]
     scales_in = [w1_scales, w2_scales, w3_scales, wo_scales]
-    n_tiles = len(TILES)
 
     with ExitStack() as ctx:
         sb = ctx.enter_context(tc.tile_pool(name="sb", bufs=1))
@@ -41,10 +45,10 @@ def tile_rows_bsoftmaxthree_kernel(
         ctx.enter_context(tc.manual_schedule())
 
         def per_tile(name):
-            return [sb.tile([P, N], F32, name="%s%d" % (name, i)) for i in range(n_tiles)]
+            return [sb.tile([P, N], F32, name="%s%d" % (name, i)) for i in range(len(TILES))]
 
         x_raw = sb.tile([P, PACK, N], F32, name="x_raw")
-        dy_raw = [sb.tile([P, PACK, HALF], F32, name="dy_raw%d" % c) for c in range(2)]
+        dy_raw = [sb.tile([P, PACK, HALF], F32, name="dy_raw%d" % c) for c in range(len(HALVES))]
         x_bf = sb.tile([P, N, PACK], BF16, name="x_bf", align_bytes=64)
         dy_bf = sb.tile([P, N, PACK], BF16, name="dy_bf", align_bytes=64)
         x_codes = sb.tile([P, N], U32, name="x_codes", align_bytes=64)
@@ -52,44 +56,57 @@ def tile_rows_bsoftmaxthree_kernel(
         x_scale = sb.tile([P, N], U8, name="x_scale", align_bytes=64)
         dy_scale = sb.tile([P, N], U8, name="dy_scale", align_bytes=64)
         w_words = [sb.tile([P, 2 * M], U8, name="w_words%d" % w, align_bytes=64) for w in range(4)]
-        w_stage = sb.tile([16, 4 * M], U8, name="w_stage", align_bytes=64)
+        w_stage = sb.tile([G * D // 32, 4 * M], U8, name="w_stage", align_bytes=64)
         w_scale = sb.tile([P, 4 * M], U8, name="w_scale", align_bytes=64)
         old_sb = [sb.tile([P, M // M_TILE, N], F32, name="old%d" % g) for g in range(G)]
         banks = [[ps.tile([P, N], F32, name="bank%d_%d" % (g, w)) for w in range(4)] for g in range(G)]
-        e1, e2, e3, th, th2 = [per_tile(name) for name in ("e1", "e2", "e3", "th", "th2")]
-        s23, se, ct, cte, cs = [per_tile(name) for name in ("s23", "se", "ct", "cte", "cs")]
-        lse, csl, rest, inv, term, res = [per_tile(name) for name in ("lse", "csl", "rest", "inv", "term", "res")]
+        e1, e2, e3, e23, se = [per_tile(name) for name in ("e1", "e2", "e3", "e23", "se")]
+        th, c_th, c_th_e1, c_slope = [per_tile(name) for name in ("th", "c_th", "c_th_e1", "c_slope")]
+        second = per_tile("second")
+        ln_se, inv_se, ln_term, rest, inv_term, result = [
+            per_tile(name) for name in ("ln_se", "inv_se", "ln_term", "rest", "inv_term", "result")
+        ]
 
-        def load_words(eng, w):
-            eng.dma_start(out=w_words[w][:].bitcast(I32), in_=words_in[w].rearrange("g p b -> (g p) b").bitcast(I32))
+
+        def load_words(w):
+            nc.sync.dma_start(
+                out=w_words[w][:].bitcast(I32), in_=words_in[w].rearrange("g p b -> (g p) b").bitcast(I32)
+            )
 
         def load_rows(tile, src):
             nc.sync.dma_start(out=tile[:], in_=src.rearrange("g (p j) n -> (g p) j n", j=PACK))
 
+        def place_scales(q):
+            nc.sync.dma_start(
+                out=w_scale[QUADRANT * q : QUADRANT * q + SCALE_ROWS, :].bitcast(I32),
+                in_=w_stage[SCALE_ROWS * q : SCALE_ROWS * (q + 1), :].bitcast(I32),
+            )
+
         nc.vector.memset(w_scale[:].bitcast(U32), 0)
-        for w, eng in ((W2, nc.sync), (W1, nc.scalar), (W3, nc.sync), (WO, nc.scalar)):
-            eng.dma_start(
+        for w, queue in ((W2, nc.sync), (W1, nc.scalar), (W3, nc.sync), (WO, nc.scalar)):
+            queue.dma_start(
                 out=w_stage[:, w * M : (w + 1) * M].bitcast(I32),
                 in_=scales_in[w].rearrange("g t m -> (g t) m").bitcast(I32),
             )
-
-        def place_scales(q):
-            nc.sync.dma_start(
-                out=w_scale[32 * q : 32 * q + 4, :].bitcast(I32), in_=w_stage[4 * q : 4 * q + 4, :].bitcast(I32)
-            )
-
         load_rows(x_raw, x)
         for w in (W2, W3, W1):
-            load_words(nc.sync, w)
+            load_words(w)
         place_scales(0)
         place_scales(1)
-        load_rows(dy_raw[0], dy[:, :, :HALF])
-        load_rows(dy_raw[1], dy[:, :, HALF:])
+        for c, cols in enumerate(HALVES):
+            load_rows(dy_raw[c], dy[:, :, cols])
+        load_words(WO)
         place_scales(2)
         place_scales(3)
-        load_words(nc.sync, WO)
         for g in range(G):
             nc.sync.dma_start(out=old_sb[g][:], in_=old[g].rearrange("(h p) n -> p h n", p=M_TILE))
+
+
+        def interleave(copy, packed, raw, cols):
+            copy(
+                out=packed[:, cols, :].rearrange("p (c i) j -> p c j i", i=RUN),
+                in_=raw.rearrange("p j (c i) -> p c j i", i=RUN),
+            )
 
         def quantize(codes, scale, packed, cols):
             nc.vector.quantize_mx(
@@ -98,12 +115,29 @@ def tile_rows_bsoftmaxthree_kernel(
                 in_=packed[:, cols, :].rearrange("p n j -> p (n j)"),
             )
 
+        for copy, cols in (
+            (nc.scalar.copy, slice(0, SCALAR_COLS)),
+            (nc.vector.tensor_copy, HALVES[1]),
+            (nc.vector.tensor_copy, slice(SCALAR_COLS, HALF)),
+        ):
+            interleave(copy, x_bf, x_raw[:, :, cols], cols)
+        for cols in reversed(HALVES):
+            quantize(x_codes, x_scale, x_bf, cols)
+        for c, cols in enumerate(HALVES):
+            interleave(nc.vector.tensor_copy, dy_bf, dy_raw[c][:], cols)
+            quantize(dy_codes, dy_scale, dy_bf, cols)
+
+
+        def bank(i, w):
+            g, h = TILES[i]
+            return banks[g][W2 if w == WO and h == 1 else w]
+
         def product(i, w):
             g, h = TILES[i]
             rows = slice(ROWS * g, ROWS * (g + 1))
             codes, scale = (dy_codes, dy_scale) if w == WO else (x_codes, x_scale)
             nc.tensor.matmul_mx(
-                out=banks[g][w][:],
+                out=bank(i, w)[:],
                 lhsT=w_words[w][rows, 2 * M_TILE * h : 2 * M_TILE * (h + 1)].bitcast(FP4X4),
                 lhsT_scale=w_scale[rows, w * M + M_TILE * h : w * M + M_TILE * (h + 1)],
                 rhs=codes[rows, :].bitcast(FP8X4),
@@ -112,104 +146,91 @@ def tile_rows_bsoftmaxthree_kernel(
                 stop=True,
             )
 
-        def forward_products(i):
-            for w in (W2, W3, W1):
-                product(i, w)
+        for i in range(len(TILES)):
+            product(i, W2)
+            product(i, W3)
+            if i >= 1:
+                product(i - 1, WO)
+            product(i, W1)
+            nc.scalar.activation(out=e2[i][:], in_=bank(i, W2)[:], func=ACT.Exp)
+            nc.scalar.activation(out=e3[i][:], in_=bank(i, W3)[:], func=ACT.Exp)
+            nc.scalar.activation(out=th[i][:], in_=bank(i, W1)[:], func=ACT.Tanh)
+            nc.scalar.activation(out=e1[i][:], in_=bank(i, W1)[:], func=ACT.Exp)
+            if i != SQUARE_ON_VECTOR:
+                nc.scalar.activation(out=second[i][:], in_=th[i][:], func=ACT.Square)
+        product(LAST, WO)
 
-        def forward(i):
-            bank = banks[TILES[i][0]]
-            nc.scalar.activation(out=e2[i][:], in_=bank[W2][:], func=ACT.Exp)
-            nc.scalar.activation(out=e3[i][:], in_=bank[W3][:], func=ACT.Exp)
-            nc.scalar.activation(out=th[i][:], in_=bank[W1][:], func=ACT.Tanh)
-            nc.scalar.activation(out=e1[i][:], in_=bank[W1][:], func=ACT.Exp)
-            if i != ON_VECTOR:
-                nc.scalar.activation(out=th2[i][:], in_=th[i][:], func=ACT.Square)
 
-        def tt(dst, a, b, op):
+        def two_inputs(dst, a, b, op):
             nc.vector.tensor_tensor(out=dst, in0=a, in1=b, op=op)
 
-        def slope(i):
-            c0 = banks[TILES[i][0]][WO]
-            if i == ON_VECTOR:
-                tt(cs[i][:], th2[i][:], c0[:], ALU.subtract)
+        def make_c_th_e1(i):
+            two_inputs(c_th_e1[i][:], c_th[i][:], e1[i][:], ALU.mult)
+
+        def make_c_slope(i):
+            if i == SQUARE_ON_VECTOR:
+                two_inputs(c_slope[i][:], second[i][:], bank(i, WO)[:], ALU.subtract)
             else:
                 nc.vector.scalar_tensor_tensor(
-                    out=cs[i][:], in0=th2[i][:], scalar=1.0, in1=c0[:], op0=ALU.subtract, op1=ALU.mult
+                    out=c_slope[i][:],
+                    in0=second[i][:],
+                    scalar=1.0,
+                    in1=bank(i, WO)[:],
+                    op0=ALU.subtract,
+                    op1=ALU.mult,
                 )
 
-        def interleave(copy, packed, raw, cols):
-            copy(
-                out=packed[:, cols, :].rearrange("p (c i) j -> p c j i", i=RUN),
-                in_=raw.rearrange("p j (c i) -> p c j i", i=RUN),
-            )
-
-        for copy, cols in (
-            (nc.scalar.copy, slice(0, SCALAR_COLS)),
-            (nc.vector.tensor_copy, slice(HALF, N)),
-            (nc.vector.tensor_copy, slice(SCALAR_COLS, HALF)),
-        ):
-            interleave(copy, x_bf, x_raw[:, :, cols], cols)
-        quantize(x_codes, x_scale, x_bf, slice(HALF, N))
-        quantize(x_codes, x_scale, x_bf, slice(0, HALF))
-        for c in range(2):
-            cols = slice(c * HALF, (c + 1) * HALF)
-            interleave(nc.vector.tensor_copy, dy_bf, dy_raw[c][:], cols)
-            quantize(dy_codes, dy_scale, dy_bf, cols)
-
-        forward_products(0)
-        for i, w in ((1, W2), (0, WO), (1, W3), (1, W1), (1, WO)):
-            product(i, w)
-        forward(0)
-        forward(1)
-        forward_products(2)
-        forward_products(3)
-        forward(2)
-        forward(3)
-        for i in range(n_tiles):
-            tt(s23[i][:], e2[i][:], e3[i][:], ALU.add)
+        for i in range(len(TILES)):
+            two_inputs(e23[i][:], e2[i][:], e3[i][:], ALU.add)
+            nc.gpsimd.tensor_tensor(out=se[i][:], in0=e23[i][:], in1=e1[i][:], op=ALU.add)
             if i >= 1:
-                nc.gpsimd.tensor_tensor(out=se[i][:], in0=s23[i][:], in1=e1[i][:], op=ALU.add)
-            tt(ct[i][:], banks[TILES[i][0]][WO][:], th[i][:], ALU.mult)
-            if i == 0:
-                tt(se[i][:], s23[i][:], e1[i][:], ALU.add)
-            else:
-                slope(i - 1)
-                if i + 1 < n_tiles:
-                    product(i + 1, WO)
-            if i == n_tiles - 1:
-                slope(i)
-            if i == ON_VECTOR:
-                tt(th2[i][:], ct[i][:], th[i][:], ALU.mult)
-            tt(cte[i][:], ct[i][:], e1[i][:], ALU.mult)
+                make_c_th_e1(i - 1)
+            two_inputs(c_th[i][:], bank(i, WO)[:], th[i][:], ALU.mult)
+            if i >= 1:
+                make_c_slope(i - 1)
+            if i == SQUARE_ON_VECTOR:
+                two_inputs(second[i][:], c_th[i][:], th[i][:], ALU.mult)
+        make_c_slope(LAST)
+        make_c_th_e1(LAST)
 
-        for i in range(n_tiles):
-            nc.scalar.activation(out=lse[i][:], in_=se[i][:], func=ACT.Ln)
-        for i in range(n_tiles):
-            nc.scalar.activation(out=inv[i][:], in_=lse[i][:], func=ACT.Exp, scale=-1.0)
 
-        def finish_rest(i):
+        for i, cols in [(0, half) for half in HALVES] + [(i, ALL) for i in range(1, len(TILES))]:
+            nc.scalar.activation(out=ln_se[i][:, cols], in_=se[i][:, cols], func=ACT.Ln)
+        for i in range(len(TILES)):
+            nc.scalar.activation(out=inv_se[i][:], in_=ln_se[i][:], func=ACT.Exp, scale=-1.0)
+
+
+        def make_ln_term(i, cols):
+            two_inputs(ln_term[i][:, cols], c_slope[i][:, cols], ln_se[i][:, cols], ALU.mult)
+
+        def make_rest(i, cols):
             g, h = TILES[i]
-            tt(rest[i][:], old_sb[g][:, h, :], csl[i][:], ALU.subtract)
+            two_inputs(rest[i][:, cols], old_sb[g][:, h, cols], ln_term[i][:, cols], ALU.subtract)
 
-        for i in range(n_tiles):
-            tt(csl[i][:], cs[i][:], lse[i][:], ALU.mult)
-            if i >= 1:
-                finish_rest(i - 1)
-        finish_rest(n_tiles - 1)
+        for cols in HALVES:
+            make_ln_term(0, cols)
+        for cols in HALVES:
+            make_rest(0, cols)
+        for i in range(1, len(TILES)):
+            make_ln_term(i, ALL)
+            if i >= 2:
+                make_rest(i - 1, ALL)
+        make_rest(LAST, ALL)
+
+        def make_inv_term(i, cols):
+            two_inputs(inv_term[i][:, cols], c_th_e1[i][:, cols], inv_se[i][:, cols], ALU.mult)
 
         def finish(i, cols):
             g, h = TILES[i]
-            tt(res[i][:, cols], term[i][:, cols], rest[i][:, cols], ALU.add)
-            nc.sync.dma_start(out=out[g, M_TILE * h : M_TILE * (h + 1), cols], in_=res[i][:, cols])
+            two_inputs(result[i][:, cols], inv_term[i][:, cols], rest[i][:, cols], ALU.add)
+            nc.sync.dma_start(out=out[g, M_TILE * h : M_TILE * (h + 1), cols], in_=result[i][:, cols])
 
-        last = n_tiles - 1
-        halves = (slice(0, HALF), slice(HALF, N))
-        for i in range(last):
-            tt(term[i][:], cte[i][:], inv[i][:], ALU.mult)
+        for i in range(LAST):
+            make_inv_term(i, ALL)
             if i >= 1:
-                finish(i - 1, slice(0, N))
-        finish(last - 1, slice(0, N))
-        for cols in halves:
-            tt(term[last][:, cols], cte[last][:, cols], inv[last][:, cols], ALU.mult)
-        for cols in halves:
-            finish(last, cols)
+                finish(i - 1, ALL)
+        finish(LAST - 1, ALL)
+        for cols in HALVES:
+            make_inv_term(LAST, cols)
+        for cols in HALVES:
+            finish(LAST, cols)

from contextlib import ExitStack

import concourse.mybir as mybir

G, D, M, N = 2, 256, 256, 512
FLOPS = 4 * 2 * G * D * M * N

F32 = mybir.dt.float32
BF16 = mybir.dt.bfloat16
I32 = mybir.dt.int32
U32 = mybir.dt.uint32
U8 = mybir.dt.uint8
FP8X4 = mybir.dt.float8_e4m3fn_x4
FP4X4 = mybir.dt.float4_e2m1fn_x4
ACT = mybir.ActivationFunctionType
ALU = mybir.AluOpType

P = 128
PACK = 4
ROWS = D // PACK
QUADRANT = 32
SCALE_ROWS = 4
M_TILE = 128
W1, W2, W3, WO = range(4)
TILES = [(g, h) for g in range(G) for h in range(M // M_TILE)]
LAST = len(TILES) - 1
HALF = N // 2
HALVES = (slice(0, HALF), slice(HALF, N))
ALL = slice(0, N)
RUN = 4
SCALAR_COLS = 176
SQUARE_ON_VECTOR = 1


def tile_rows_bsoftmaxthree_kernel(
    tc, x, w1_words, w1_scales, w2_words, w2_scales, w3_words, w3_scales, wo_words, wo_scales, dy, old, out
):
    nc = tc.nc
    words_in = [w1_words, w2_words, w3_words, wo_words]
    scales_in = [w1_scales, w2_scales, w3_scales, wo_scales]

    with ExitStack() as ctx:
        sb = ctx.enter_context(tc.tile_pool(name="sb", bufs=1))
        ps = ctx.enter_context(tc.psum_pool(name="ps", bufs=1))
        ctx.enter_context(tc.manual_schedule())

        def per_tile(name):
            return [sb.tile([P, N], F32, name="%s%d" % (name, i)) for i in range(len(TILES))]

        x_raw = sb.tile([P, PACK, N], F32, name="x_raw")
        dy_raw = [sb.tile([P, PACK, HALF], F32, name="dy_raw%d" % c) for c in range(len(HALVES))]
        x_bf = sb.tile([P, N, PACK], BF16, name="x_bf", align_bytes=64)
        dy_bf = sb.tile([P, N, PACK], BF16, name="dy_bf", align_bytes=64)
        x_codes = sb.tile([P, N], U32, name="x_codes", align_bytes=64)
        dy_codes = sb.tile([P, N], U32, name="dy_codes", align_bytes=64)
        x_scale = sb.tile([P, N], U8, name="x_scale", align_bytes=64)
        dy_scale = sb.tile([P, N], U8, name="dy_scale", align_bytes=64)
        w_words = [sb.tile([P, 2 * M], U8, name="w_words%d" % w, align_bytes=64) for w in range(4)]
        w_stage = sb.tile([G * D // 32, 4 * M], U8, name="w_stage", align_bytes=64)
        w_scale = sb.tile([P, 4 * M], U8, name="w_scale", align_bytes=64)
        old_sb = [sb.tile([P, M // M_TILE, N], F32, name="old%d" % g) for g in range(G)]
        banks = [[ps.tile([P, N], F32, name="bank%d_%d" % (g, w)) for w in range(4)] for g in range(G)]
        e1, e2, e3, e23, se = [per_tile(name) for name in ("e1", "e2", "e3", "e23", "se")]
        th, c_th, c_th_e1, c_slope = [per_tile(name) for name in ("th", "c_th", "c_th_e1", "c_slope")]
        second = per_tile("second")
        ln_se, inv_se, ln_term, rest, inv_term, result = [
            per_tile(name) for name in ("ln_se", "inv_se", "ln_term", "rest", "inv_term", "result")
        ]


        def load_words(w):
            nc.sync.dma_start(
                out=w_words[w][:].bitcast(I32), in_=words_in[w].rearrange("g p b -> (g p) b").bitcast(I32)
            )

        def load_rows(tile, src):
            nc.sync.dma_start(out=tile[:], in_=src.rearrange("g (p j) n -> (g p) j n", j=PACK))

        def place_scales(q):
            nc.sync.dma_start(
                out=w_scale[QUADRANT * q : QUADRANT * q + SCALE_ROWS, :].bitcast(I32),
                in_=w_stage[SCALE_ROWS * q : SCALE_ROWS * (q + 1), :].bitcast(I32),
            )

        nc.vector.memset(w_scale[:].bitcast(U32), 0)
        for w, queue in ((W2, nc.sync), (W1, nc.scalar), (W3, nc.sync), (WO, nc.scalar)):
            queue.dma_start(
                out=w_stage[:, w * M : (w + 1) * M].bitcast(I32),
                in_=scales_in[w].rearrange("g t m -> (g t) m").bitcast(I32),
            )
        load_rows(x_raw, x)
        for w in (W2, W3, W1):
            load_words(w)
        place_scales(0)
        place_scales(1)
        for c, cols in enumerate(HALVES):
            load_rows(dy_raw[c], dy[:, :, cols])
        load_words(WO)
        place_scales(2)
        place_scales(3)
        for g in range(G):
            nc.sync.dma_start(out=old_sb[g][:], in_=old[g].rearrange("(h p) n -> p h n", p=M_TILE))


        def interleave(copy, packed, raw, cols):
            copy(
                out=packed[:, cols, :].rearrange("p (c i) j -> p c j i", i=RUN),
                in_=raw.rearrange("p j (c i) -> p c j i", i=RUN),
            )

        def quantize(codes, scale, packed, cols):
            nc.vector.quantize_mx(
                out=codes[:, cols].bitcast(FP8X4),
                scales=scale[:, cols],
                in_=packed[:, cols, :].rearrange("p n j -> p (n j)"),
            )

        for copy, cols in (
            (nc.scalar.copy, slice(0, SCALAR_COLS)),
            (nc.vector.tensor_copy, HALVES[1]),
            (nc.vector.tensor_copy, slice(SCALAR_COLS, HALF)),
        ):
            interleave(copy, x_bf, x_raw[:, :, cols], cols)
        for cols in reversed(HALVES):
            quantize(x_codes, x_scale, x_bf, cols)
        for c, cols in enumerate(HALVES):
            interleave(nc.vector.tensor_copy, dy_bf, dy_raw[c][:], cols)
            quantize(dy_codes, dy_scale, dy_bf, cols)


        def bank(i, w):
            g, h = TILES[i]
            return banks[g][W2 if w == WO and h == 1 else w]

        def product(i, w):
            g, h = TILES[i]
            rows = slice(ROWS * g, ROWS * (g + 1))
            codes, scale = (dy_codes, dy_scale) if w == WO else (x_codes, x_scale)
            nc.tensor.matmul_mx(
                out=bank(i, w)[:],
                lhsT=w_words[w][rows, 2 * M_TILE * h : 2 * M_TILE * (h + 1)].bitcast(FP4X4),
                lhsT_scale=w_scale[rows, w * M + M_TILE * h : w * M + M_TILE * (h + 1)],
                rhs=codes[rows, :].bitcast(FP8X4),
                rhs_scale=scale[rows, :],
                start=True,
                stop=True,
            )

        for i in range(len(TILES)):
            product(i, W2)
            product(i, W3)
            if i >= 1:
                product(i - 1, WO)
            product(i, W1)
            nc.scalar.activation(out=e2[i][:], in_=bank(i, W2)[:], func=ACT.Exp)
            nc.scalar.activation(out=e3[i][:], in_=bank(i, W3)[:], func=ACT.Exp)
            nc.scalar.activation(out=th[i][:], in_=bank(i, W1)[:], func=ACT.Tanh)
            nc.scalar.activation(out=e1[i][:], in_=bank(i, W1)[:], func=ACT.Exp)
            if i != SQUARE_ON_VECTOR:
                nc.scalar.activation(out=second[i][:], in_=th[i][:], func=ACT.Square)
        product(LAST, WO)


        def two_inputs(dst, a, b, op):
            nc.vector.tensor_tensor(out=dst, in0=a, in1=b, op=op)

        def make_c_th_e1(i):
            two_inputs(c_th_e1[i][:], c_th[i][:], e1[i][:], ALU.mult)

        def make_c_slope(i):
            if i == SQUARE_ON_VECTOR:
                two_inputs(c_slope[i][:], second[i][:], bank(i, WO)[:], ALU.subtract)
            else:
                nc.vector.scalar_tensor_tensor(
                    out=c_slope[i][:],
                    in0=second[i][:],
                    scalar=1.0,
                    in1=bank(i, WO)[:],
                    op0=ALU.subtract,
                    op1=ALU.mult,
                )

        for i in range(len(TILES)):
            two_inputs(e23[i][:], e2[i][:], e3[i][:], ALU.add)
            nc.gpsimd.tensor_tensor(out=se[i][:], in0=e23[i][:], in1=e1[i][:], op=ALU.add)
            if i >= 1:
                make_c_th_e1(i - 1)
            two_inputs(c_th[i][:], bank(i, WO)[:], th[i][:], ALU.mult)
            if i >= 1:
                make_c_slope(i - 1)
            if i == SQUARE_ON_VECTOR:
                two_inputs(second[i][:], c_th[i][:], th[i][:], ALU.mult)
        make_c_slope(LAST)
        make_c_th_e1(LAST)


        for i, cols in [(0, half) for half in HALVES] + [(i, ALL) for i in range(1, len(TILES))]:
            nc.scalar.activation(out=ln_se[i][:, cols], in_=se[i][:, cols], func=ACT.Ln)
        for i in range(len(TILES)):
            nc.scalar.activation(out=inv_se[i][:], in_=ln_se[i][:], func=ACT.Exp, scale=-1.0)


        def make_ln_term(i, cols):
            two_inputs(ln_term[i][:, cols], c_slope[i][:, cols], ln_se[i][:, cols], ALU.mult)

        def make_rest(i, cols):
            g, h = TILES[i]
            two_inputs(rest[i][:, cols], old_sb[g][:, h, cols], ln_term[i][:, cols], ALU.subtract)

        for cols in HALVES:
            make_ln_term(0, cols)
        for cols in HALVES:
            make_rest(0, cols)
        for i in range(1, len(TILES)):
            make_ln_term(i, ALL)
            if i >= 2:
                make_rest(i - 1, ALL)
        make_rest(LAST, ALL)

        def make_inv_term(i, cols):
            two_inputs(inv_term[i][:, cols], c_th_e1[i][:, cols], inv_se[i][:, cols], ALU.mult)

        def finish(i, cols):
            g, h = TILES[i]
            two_inputs(result[i][:, cols], inv_term[i][:, cols], rest[i][:, cols], ALU.add)
            nc.sync.dma_start(out=out[g, M_TILE * h : M_TILE * (h + 1), cols], in_=result[i][:, cols])

        for i in range(LAST):
            make_inv_term(i, ALL)
            if i >= 1:
                finish(i - 1, ALL)
        finish(LAST - 1, ALL)
        for cols in HALVES:
            make_inv_term(LAST, cols)
        for cols in HALVES:
            finish(LAST, cols)
